import numpy as np
import ml_dtypes


def mxq(x, axis, fmt="e4m3"):
    dtype, down = {"e4m3": (ml_dtypes.float8_e4m3fn, 7), "e5m2": (ml_dtypes.float8_e5m2, 14)}[fmt]
    v = np.moveaxis(np.asarray(x, np.float32).astype(ml_dtypes.bfloat16).astype(np.float64), axis, -1)
    blocks = v.reshape(v.shape[:-1] + (-1, 32))
    amax = np.abs(blocks).max(-1, keepdims=True)
    byte = np.maximum(np.where(amax > 0, np.frexp(amax)[1] - 1 + 127, 0) - down, 1)
    scale = np.exp2(byte - 127.0)
    codes = (blocks / scale).astype(np.float32).astype(dtype).astype(np.float64)
    return np.moveaxis((codes * scale).reshape(v.shape), -1, axis)


WIDE = False


def mx_kscale(k):
    if not WIDE:
        return np.ones(k)
    levels = np.array([10, -10, 5, -5, 0])
    if k % 512:
        return np.exp2(np.random.permutation(np.resize(levels, k // 32))).repeat(32)
    a = np.empty((k // 512, 16))
    for p in range(k // 512):
        a[p, :8] = np.random.permutation(np.resize(levels, 8))
        for g in range(8):
            far = levels[np.abs(levels - a[p, g]) >= 10]
            a[p, g + 8] = far[np.random.randint(len(far))]
    return np.exp2(a.ravel()).repeat(32)


def f64(x):
    return np.asarray(x).astype(np.float64)


def striped(idx):
    return np.tile(np.asarray(idx).reshape(-1, 16).T, (8, 1)).astype(np.uint16)


def unstriped(offs):
    return offs[:16].T.reshape(-1).astype(np.int64)


E2M1 = np.array([0.0, 0.5, 1.0, 1.5, 2.0, 3.0, 4.0, 6.0, -0.0, -0.5, -1.0, -1.5, -2.0, -3.0, -4.0, -6.0])


def pack_weight(w, fmt):
    k, n = w.shape
    w = f64(np.asarray(w, np.float32).astype(ml_dtypes.bfloat16)).reshape(k // 32, 32, n)
    amax = np.abs(w).max(1)
    if fmt == "e4m3":
        byte = np.frexp(amax)[1] - 1 + 127 - 7
    else:
        mant, ex = np.frexp(amax / 6.0)
        byte = np.where(mant > 0.5, ex, ex - 1) + 127
    byte = np.clip(np.where(amax > 0, byte, 1), 1, 254)
    scaled = (w * np.exp2(127.0 - byte)[:, None, :]).reshape(k, n).astype(np.float32)
    by_word = np.ascontiguousarray(scaled.reshape(k // 512, 128, 4, n).transpose(0, 1, 3, 2))
    if fmt == "e4m3":
        words = by_word.astype(ml_dtypes.float8_e4m3fn).view(np.uint8)
    else:
        c = by_word.astype(ml_dtypes.float4_e2m1fn).view(np.uint8) & 0xF
        words = (c[..., 0::2] | (c[..., 1::2] << 4)).reshape(k // 512, 128, 2 * n)
    return np.ascontiguousarray(words), np.ascontiguousarray(byte.astype(np.uint8).reshape(k // 512, 16, n))


def unpack_weight(words, scales, fmt):
    g, _, n = scales.shape
    words = np.ascontiguousarray(words).reshape(g, 128, n, -1)
    if fmt == "e4m3":
        vals = words.view(ml_dtypes.float8_e4m3fn).astype(np.float64)
    else:
        nib = np.empty((g, 128, n, 4), np.uint8)
        nib[..., 0::2] = words & 0xF
        nib[..., 1::2] = words >> 4
        vals = E2M1[nib]
    vals = vals * np.repeat(np.exp2(scales.astype(np.float64) - 127.0), 8, axis=1)[..., None]
    return vals.transpose(0, 1, 3, 2).reshape(g * 512, n)


D, E, T, I, Q, G = 512, 512, 2048, 512, 128, 64


def setup_inputs():
    n = np.random.standard_normal
    idx = np.random.permutation(T)[:I]
    fd = mx_kscale(D)
    fe = mx_kscale(E)
    keysp = pack_weight(n((D, T)) / fd[:, None], "e2m1")
    valsp = pack_weight(n((E, T)) / fe[:, None], "e2m1")
    return {
        "query": (n((D, Q)) * 0.6 / np.sqrt(D) * fd[:, None]).astype(np.float32),
        "keys_words": keysp[0],
        "keys_scales": keysp[1],
        "pen": (np.random.uniform(10.0, 40.0, (Q, 1))).astype(np.float32),
        "gout": (n((E, Q)) * 1 / np.sqrt(E) * fe[:, None]).astype(np.float32),
        "vals_words": valsp[0],
        "vals_scales": valsp[1],
        "dquery": (n((D, Q)) * 1.0 / np.sqrt(D) * fd[:, None]).astype(np.float32),
        "base": (0.5 * n((Q, T))).astype(np.float32),
        "offs": striped(idx),
    }


def reference(query, keys_words, keys_scales, pen, gout, vals_words, vals_scales, dquery, base, offs):
    idx = unstriped(offs)
    keysu = unpack_weight(keys_words, keys_scales, "e2m1")
    valsu = unpack_weight(vals_words, vals_scales, "e2m1")
    queryq = mxq(f64(query), 0, "e4m3")
    keysidxg = keysu[:, idx]
    a = queryq.T @ keysidxg
    dqueryq = mxq(f64(dquery), 0, "e4m3")
    ta = dqueryq.T @ keysidxg
    p = np.exp(a - np.max(a, axis=1, keepdims=True))
    z = np.sum(p, axis=1, keepdims=True)
    goutq = mxq(f64(gout), 0, "e4m3")
    valsidxg = valsu[:, idx]
    c0 = goutq.T @ valsidxg
    s = p.reshape(Q, G, I // G).sum(axis=2) / z
    ds = f64(pen) * (-1.0) * s * 2.0
    e1 = ds / z
    r1 = np.repeat(e1, I // G, axis=1)
    dz = np.sum(ds * p.reshape(Q, G, I // G).sum(axis=2) / np.square(z) * (-1.0), axis=1, keepdims=True) - np.sum(p * c0, axis=1, keepdims=True) / np.square(z)
    dp = 1.0 / z * c0 + r1 + dz
    tp = ta * p
    tz = np.sum(tp, axis=1, keepdims=True)
    ts = (tp.reshape(Q, G, I // G).sum(axis=2) - tz * p.reshape(Q, G, I // G).sum(axis=2) / z) / z
    tds = ts * f64(pen) * (-1.0) * 2.0
    te1 = (tds - tz * ds / z) / z
    tr1 = np.repeat(te1, I // G, axis=1)
    tdz = np.sum((tds * p.reshape(Q, G, I // G).sum(axis=2) + tp.reshape(Q, G, I // G).sum(axis=2) * ds - tz * z * 2.0 * ds * p.reshape(Q, G, I // G).sum(axis=2) / np.square(z)) / np.square(z) * (-1.0), axis=1, keepdims=True) - (np.sum(tp * c0, axis=1, keepdims=True) - tz * z * 2.0 * np.sum(p * c0, axis=1, keepdims=True) / np.square(z)) / np.square(z)
    tdp = tz * 1.0 / np.square(z) * (-1.0) * c0 + tr1 + tdz
    tda = tdp * p + tp * dp
    gs = tda * 512.0
    gf = np.zeros((Q, T))
    gf[:, idx] = gs
    y = f64(base) + gf
    return y

@@ -1,0 +1,189 @@
+from contextlib import ExitStack
+
+import concourse.mybir as mybir
+
+F32 = mybir.dt.float32
+BF16 = mybir.dt.bfloat16
+I32 = mybir.dt.int32
+U32 = mybir.dt.uint32
+U16 = mybir.dt.uint16
+U8 = mybir.dt.uint8
+FP8X4 = mybir.dt.float8_e4m3fn_x4
+FP4X4 = mybir.dt.float4_e2m1fn_x4
+ALU = mybir.AluOpType
+ACT = mybir.ActivationFunctionType
+AXIS = mybir.AxisListType
+
+P = 128
+PACK = 4
+D, T, SLOTS, Q, PAGES = 512, 2048, 512, 128, 64
+PAGE = SLOTS // PAGES
+GAIN = 512.0
+FLOPS = 3 * 2 * D * Q * SLOTS
+
+
+def tile_attend_hvcrowding_s_kernel(tc, query, keys_words, keys_scales, pen, gout, vals_words, vals_scales, dquery, base, offs, out):
+    nc = tc.nc
+    with ExitStack() as ctx:
+        sb = ctx.enter_context(tc.tile_pool(name="sb", bufs=1))
+        ps = ctx.enter_context(tc.psum_pool(name="ps", bufs=1))
+
+        def tile(name, shape, dtype, tag=None):
+            return sb.tile(shape, dtype, name=name, tag=tag or name, align_bytes=64)
+
+        offsets = tile("offsets", [P, SLOTS // 16], U16)
+        k_words = tile("k_words", [P, T], U16)
+        k_scales = tile("k_scales", [P, T], U8)
+        v_scales = tile("v_scales", [P, T], U8)
+        window = tile("window", [P, T], F32)
+        result = tile("result", [P, T], F32)
+        pen_sb = tile("pen_sb", [P, 1], F32)
+        warm_in = tile("warm_in", [P, 1], F32)
+        warm_out = tile("warm_out", [P, 1], F32)
+
+        nc.vector.memset(k_scales[:].bitcast(I32), 0)
+        nc.vector.memset(window[:], 0.0)
+        nc.vector.memset(v_scales[:].bitcast(I32), 0)
+        nc.gpsimd.memset(warm_in[:], 0.0)
+        warm_sum = tile("warm_sum", [P, 1], F32)
+        nc.scalar.activation(out=warm_out[:], in_=warm_in[:], func=ACT.Exp, accum_out=warm_sum[:])
+
+        def load_rows(name, src, tag=None):
+            raw = tile(name, [P, PACK, Q], F32, tag)
+            nc.sync.dma_start(out=raw[:], in_=src.rearrange("(p j) q -> p j q", j=PACK))
+            return raw
+
+        def load_scales(dst, src):
+            for quad in range(4):
+                nc.sync.dma_start(out=dst[32 * quad : 32 * quad + 4, :].bitcast(I32), in_=src[0, 4 * quad : 4 * quad + 4, :].bitcast(I32))
+
+        nc.gpsimd.dma_start(out=pen_sb[:], in_=pen)
+        nc.sync.dma_start(offsets[:], offs)
+        nc.sync.dma_start(out=k_words[:].bitcast(I32), in_=keys_words[0].bitcast(I32))
+        q_raw = load_rows("q_raw", query)
+        load_scales(k_scales, keys_scales)
+        dq_raw = load_rows("dq_raw", dquery, "warm_out")
+        v_words = tile("v_words", [P, T], U16, "warm_in")
+        nc.sync.dma_start(out=v_words[:].bitcast(I32), in_=vals_words[0].bitcast(I32))
+        g_raw = load_rows("g_raw", gout, "warm_sum")
+        load_scales(v_scales, vals_scales)
+
+        def interleave(grouped, raw):
+            nc.scalar.copy(out=grouped.rearrange("p (q j) -> p q j", j=PACK), in_=raw[:].rearrange("p j q -> p q j"))
+
+        def quantize(name, grouped, width):
+            codes = tile(name + "_codes", [P, width], U32)
+            scales = tile(name + "_scales", [P, width], U8)
+            nc.vector.quantize_mx(out=codes[:].bitcast(FP8X4), scales=scales[:], in_=grouped[:])
+            return [(codes[:, c : c + Q], scales[:, c : c + Q]) for c in range(0, width, Q)]
+
+        def gather(name, pool, dtype):
+            picked = tile(name, [P, SLOTS], dtype)
+            nc.vector.tensor_copy(picked[:], pool[:].indirect(offsets[:]))
+            return picked
+
+        def product(name, rows, words, scales):
+            acc = ps.tile([P, SLOTS], F32, name=name)
+            nc.tensor.matmul_mx(out=acc[:], lhsT=rows[0].bitcast(FP8X4), lhsT_scale=rows[1], rhs=words[:].bitcast(FP4X4), rhs_scale=scales[:], start=True, stop=True)
+            return acc
+
+        def col(name):
+            return tile(name, [P, 1], F32)
+
+        def paged(ap):
+            return ap.rearrange("p (g j) -> p g j", j=PAGE)
+
+        def spread(ap):
+            return ap.unsqueeze(2).to_broadcast([P, ap.shape[1], PAGE])
+
+        q_bf = tile("q_bf", [P, Q * PACK], BF16)
+        dg_bf = tile("dg_bf", [P, 2 * Q * PACK], BF16)
+        interleave(q_bf[:], q_raw)
+        interleave(dg_bf[:, : Q * PACK], dq_raw)
+        interleave(dg_bf[:, Q * PACK :], g_raw)
+
+        kw = gather("kw", k_words, U16)
+        ks = gather("ks", k_scales, U8)
+        base_sb = tile("base_sb", [P, T], F32, "k_scales")
+        nc.sync.dma_start(out=base_sb[:], in_=base)
+        (q_mx,) = quantize("q", q_bf, Q)
+        a = product("a", q_mx, kw, ks)
+        vw = gather("vw", v_words, U16)
+        neg_max = tile("neg_max", [P, 1], F32, "warm_in")
+        nc.vector.tensor_reduce(out=neg_max[:], in_=a[:], axis=AXIS.X, op=ALU.max, negate=True)
+        p = tile("p", [P, SLOTS], F32, "warm_sum")
+        z = col("z")
+        nc.scalar.activation(out=p[:], in_=a[:], func=ACT.Exp, bias=neg_max[:], scale=1.0, accum_out=z[:])
+        vs = gather("vs", v_scales, U8)
+        dq_mx, g_mx = quantize("dg", dg_bf, 2 * Q)
+        ta = product("ta", dq_mx, kw, ks)
+        c0 = product("c0", g_mx, vw, vs)
+
+        held = tile("held", [P, SLOTS + PAGES + 1], F32, "v_scales")
+        tp = held[:, :SLOTS]
+        p_page = held[:, SLOTS : SLOTS + PAGES]
+        rz = held[:, SLOTS + PAGES :]
+        nc.vector.reciprocal(out=rz, in_=z[:])
+        nc.vector.tensor_reduce(out=p_page, in_=paged(p[:]), axis=AXIS.X, op=ALU.add)
+        tz = col("tz")
+        nc.vector.scalar_tensor_tensor(out=tp, in0=ta[:], scalar=1.0, in1=p[:], op0=ALU.mult, op1=ALU.mult, accum_out=tz[:])
+
+        k = col("k")
+        nc.scalar.activation(out=k[:], in_=pen_sb[:], func=ACT.Copy, scale=-2.0)
+        kr = col("kr")
+        nc.scalar.activation(out=kr[:], in_=k[:], func=ACT.Copy, scale=rz)
+        m = col("m")
+        nc.scalar.activation(out=m[:], in_=tz[:], func=ACT.Copy, scale=rz)
+        krp = tile("krp", [P, PAGES], F32)
+        nc.scalar.activation(out=krp[:], in_=p_page, func=ACT.Copy, scale=kr[:])
+        p_sq = tile("p_sq", [P, PAGES], F32)
+        sp2 = col("sp2")
+        nc.scalar.activation(out=p_sq[:], in_=p_page, func=ACT.Square, accum_out=sp2[:])
+
+        pc = tile("pc", [P, SLOTS], F32)
+        c_sum = col("c_sum")
+        nc.vector.scalar_tensor_tensor(out=pc[:], in0=c0[:], scalar=1.0, in1=p[:], op0=ALU.mult, op1=ALU.mult, accum_out=c_sum[:])
+        tp_page = tile("tp_page", [P, PAGES], F32)
+        nc.vector.tensor_reduce(out=tp_page[:], in_=paged(tp), axis=AXIS.X, op=ALU.add)
+
+        a_sum = col("a_sum")
+        nc.scalar.activation(out=a_sum[:], in_=sp2[:], func=ACT.Identity, scale=kr[:], bias=c_sum[:])
+        a0 = col("a0")
+        nc.scalar.activation(out=a0[:], in_=a_sum[:], func=ACT.Copy, scale=rz)
+
+        x1 = tile("x1", [P, SLOTS], F32)
+        nc.vector.scalar_tensor_tensor(out=paged(x1[:]), in0=paged(c0[:]), scalar=a0[:], in1=spread(krp[:]), op0=ALU.subtract, op1=ALU.add)
+        neg_g = tile("neg_g", [P, PAGES], F32)
+        nc.vector.scalar_tensor_tensor(out=neg_g[:], in0=p_page, scalar=m[:], in1=tp_page[:], op0=ALU.mult, op1=ALU.subtract)
+        y = tile("y", [P, SLOTS], F32)
+        e_sum = col("e_sum")
+        nc.vector.scalar_tensor_tensor(out=y[:], in0=ta[:], scalar=m[:], in1=pc[:], op0=ALU.subtract, op1=ALU.mult, accum_out=e_sum[:])
+        gp = tile("gp", [P, PAGES], F32)
+        q2 = col("q2")
+        nc.vector.scalar_tensor_tensor(out=gp[:], in0=neg_g[:], scalar=-2.0, in1=krp[:], op0=ALU.mult, op1=ALU.mult, accum_out=q2[:])
+        x2 = tile("x2", [P, SLOTS], F32)
+        halves = [slice(0, SLOTS // 2), slice(SLOTS // 2, SLOTS)]
+        for h in halves:
+            nc.vector.scalar_tensor_tensor(out=x2[:, h], in0=ta[:, h], scalar=m[:], in1=x1[:, h], op0=ALU.subtract, op1=ALU.mult)
+
+        neg_krg = tile("neg_krg", [P, PAGES], F32)
+        nc.scalar.activation(out=neg_krg[:], in_=neg_g[:], func=ACT.Copy, scale=kr[:])
+        b_sum = col("b_sum")
+        nc.scalar.activation(out=b_sum[:], in_=q2[:], func=ACT.Identity, scale=1.0, bias=e_sum[:])
+        b0 = col("b0")
+        nc.scalar.activation(out=b0[:], in_=b_sum[:], func=ACT.Copy, scale=rz)
+        gain = col("gain")
+        nc.scalar.activation(out=gain[:], in_=rz, func=ACT.Copy, scale=GAIN)
+        w = tile("w", [P, SLOTS], F32)
+        nc.scalar.activation(out=w[:], in_=p[:], func=ACT.Copy, scale=gain[:])
+
+        x3 = tile("x3", [P, SLOTS], F32)
+        for h in halves:
+            nc.vector.scalar_tensor_tensor(out=paged(x3[:, h]), in0=paged(x2[:, h]), scalar=b0[:], in1=spread(neg_krg[:, h.start // PAGE : h.stop // PAGE]), op0=ALU.subtract, op1=ALU.subtract)
+        nc.vector.tensor_tensor(window[:].indirect(offsets[:]), x3[:], w[:], ALU.mult)
+
+        edges = [0, 256, 768, 1280, 1792, 2048]
+        for c in range(5):
+            cols = slice(edges[c], edges[c + 1])
+            nc.vector.tensor_tensor(result[:, cols], window[:, cols], base_sb[:, cols], ALU.add)
+            nc.sync.dma_start(out=out[:, cols], in_=result[:, cols])

@@ -37,7 +37,6 @@ def tile_attend_hvcrowding_s_kernel(tc, query, keys_words, keys_scales, pen, gou
         v_scales = tile("v_scales", [P, T], U8)
         window = tile("window", [P, T], F32)
         result = tile("result", [P, T], F32)
-        pen_sb = tile("pen_sb", [P, 1], F32)
         warm_in = tile("warm_in", [P, 1], F32)
         warm_out = tile("warm_out", [P, 1], F32)
 
@@ -54,17 +53,16 @@ def tile_attend_hvcrowding_s_kernel(tc, query, keys_words, keys_scales, pen, gou
             return raw
 
         def load_scales(dst, src):
-            for quad in range(4):
-                nc.sync.dma_start(out=dst[32 * quad : 32 * quad + 4, :].bitcast(I32), in_=src[0, 4 * quad : 4 * quad + 4, :].bitcast(I32))
+            for r in range(4):
+                nc.sync.dma_start(out=dst[r:P:32, :].bitcast(I32), in_=src[0, r:16:4, :].bitcast(I32))
 
-        nc.gpsimd.dma_start(out=pen_sb[:], in_=pen)
         nc.sync.dma_start(offsets[:], offs)
         nc.sync.dma_start(out=k_words[:].bitcast(I32), in_=keys_words[0].bitcast(I32))
         q_raw = load_rows("q_raw", query)
         load_scales(k_scales, keys_scales)
-        dq_raw = load_rows("dq_raw", dquery, "warm_out")
         v_words = tile("v_words", [P, T], U16, "warm_in")
         nc.sync.dma_start(out=v_words[:].bitcast(I32), in_=vals_words[0].bitcast(I32))
+        dq_raw = load_rows("dq_raw", dquery, "warm_out")
         g_raw = load_rows("g_raw", gout, "warm_sum")
         load_scales(v_scales, vals_scales)
 
@@ -99,6 +97,8 @@ def tile_attend_hvcrowding_s_kernel(tc, query, keys_words, keys_scales, pen, gou
         q_bf = tile("q_bf", [P, Q * PACK], BF16)
         dg_bf = tile("dg_bf", [P, 2 * Q * PACK], BF16)
         interleave(q_bf[:], q_raw)
+        pen_sb = tile("pen_sb", [P, 1], F32, "q_raw")
+        nc.sync.dma_start(out=pen_sb[:], in_=pen)
         interleave(dg_bf[:, : Q * PACK], dq_raw)
         interleave(dg_bf[:, Q * PACK :], g_raw)
 

@@ -16,174 +16,216 @@ AXIS = mybir.AxisListType
 
 P = 128
 PACK = 4
-D, T, SLOTS, Q, PAGES = 512, 2048, 512, 128, 64
+QUADRANT = 32
+SCALE_ROWS = 16
+LIST_ROWS = 16
+FEATURES = 512
+TOKENS = 2048
+SLOTS = 512
+ROWS = 128
+PAGES = 64
 PAGE = SLOTS // PAGES
 GAIN = 512.0
-FLOPS = 3 * 2 * D * Q * SLOTS
+HALVES = (slice(0, SLOTS // 2), slice(SLOTS // 2, SLOTS))
+STORE_EDGES = (0, 256, 768, 1280, 1792, 2048)
+FIRST_CLEAR = 256
+
+FLOPS = 3 * 2 * FEATURES * ROWS * SLOTS
 
 
 def tile_attend_hvcrowding_s_kernel(tc, query, keys_words, keys_scales, pen, gout, vals_words, vals_scales, dquery, base, offs, out):
     nc = tc.nc
     with ExitStack() as ctx:
-        sb = ctx.enter_context(tc.tile_pool(name="sb", bufs=1))
-        ps = ctx.enter_context(tc.psum_pool(name="ps", bufs=1))
+        sbuf = ctx.enter_context(tc.tile_pool(name="sbuf", bufs=1))
+        psum = ctx.enter_context(tc.psum_pool(name="psum", bufs=1))
 
-        def tile(name, shape, dtype, tag=None):
-            return sb.tile(shape, dtype, name=name, tag=tag or name, align_bytes=64)
+        def tile(name, width, dtype=F32, on=None):
+            return sbuf.tile([P] + width, dtype, name=name, tag=on or name, align_bytes=64)
 
-        offsets = tile("offsets", [P, SLOTS // 16], U16)
-        k_words = tile("k_words", [P, T], U16)
-        k_scales = tile("k_scales", [P, T], U8)
-        v_scales = tile("v_scales", [P, T], U8)
-        window = tile("window", [P, T], F32)
-        result = tile("result", [P, T], F32)
-        warm_in = tile("warm_in", [P, 1], F32)
-        warm_out = tile("warm_out", [P, 1], F32)
+        def paged(ap):
+            return ap.rearrange("p (g j) -> p g j", j=PAGE)
+
+        def per_slot(page_values, half):
+            pages = page_values[:, half.start // PAGE : half.stop // PAGE]
+            return pages.unsqueeze(2).to_broadcast([P, PAGES // 2, PAGE])
+
+        def scaled(name, width, src, scale, on=None):
+            dst = tile(name, [width], on=on)
+            nc.scalar.activation(out=dst[:], in_=src, func=ACT.Copy, scale=scale)
+            return dst
+
+        def affine(name, src, scale, bias):
+            dst = tile(name, [1])
+            nc.scalar.activation(out=dst[:], in_=src, func=ACT.Identity, scale=scale, bias=bias)
+            return dst
+
+        offsets = tile("offsets", [SLOTS // LIST_ROWS], U16)
+        k_words = tile("k_words", [TOKENS], U16)
+        k_scales = tile("k_scales", [TOKENS], U8)
+        v_scales = tile("v_scales", [TOKENS], U8)
+        window = tile("window", [TOKENS])
+        result = tile("result", [TOKENS])
 
         nc.vector.memset(k_scales[:].bitcast(I32), 0)
-        nc.vector.memset(window[:], 0.0)
+        constants = [2.0, GAIN, 1.0 / PAGES, 1.0, -1.0 / PAGES]
+        seed = tile("seed", [len(constants)])
+        for c, value in enumerate(constants):
+            nc.vector.memset(seed[:, c : c + 1], value)
+        factors = tile("factors", [2 + len(constants)])
+        nc.vector.tensor_copy(factors[:, 2:], seed[:])
+        nc.vector.memset(window[:, :FIRST_CLEAR], 0.0)
+        nc.vector.memset(window[:, FIRST_CLEAR:], 0.0)
         nc.vector.memset(v_scales[:].bitcast(I32), 0)
+
+        warm_in = tile("warm_in", [1])
+        warm_out = tile("warm_out", [1])
+        warm_sum = tile("warm_sum", [1])
         nc.gpsimd.memset(warm_in[:], 0.0)
-        warm_sum = tile("warm_sum", [P, 1], F32)
         nc.scalar.activation(out=warm_out[:], in_=warm_in[:], func=ACT.Exp, accum_out=warm_sum[:])
 
-        def load_rows(name, src, tag=None):
-            raw = tile(name, [P, PACK, Q], F32, tag)
-            nc.sync.dma_start(out=raw[:], in_=src.rearrange("(p j) q -> p j q", j=PACK))
-            return raw
+        def load_words(dst, src):
+            nc.sync.dma_start(out=dst[:].bitcast(I32), in_=src[0].bitcast(I32))
 
         def load_scales(dst, src):
-            for r in range(4):
-                nc.sync.dma_start(out=dst[r:P:32, :].bitcast(I32), in_=src[0, r:16:4, :].bitcast(I32))
+            for r in range(PACK):
+                nc.sync.dma_start(out=dst[r:P:QUADRANT, :].bitcast(I32), in_=src[0, r:SCALE_ROWS:PACK, :].bitcast(I32))
+
+        def load_rows(name, src, on):
+            raw = tile(name, [PACK, ROWS], on=on)
+            nc.sync.dma_start(out=raw[:], in_=src.rearrange("(p t) q -> p t q", t=PACK))
+            return raw
 
         nc.sync.dma_start(offsets[:], offs)
-        nc.sync.dma_start(out=k_words[:].bitcast(I32), in_=keys_words[0].bitcast(I32))
-        q_raw = load_rows("q_raw", query)
+        load_words(k_words, keys_words)
         load_scales(k_scales, keys_scales)
-        v_words = tile("v_words", [P, T], U16, "warm_in")
-        nc.sync.dma_start(out=v_words[:].bitcast(I32), in_=vals_words[0].bitcast(I32))
+        q_raw = load_rows("q_raw", query, "seed")
+        v_words = tile("v_words", [TOKENS], U16, on="warm_in")
+        load_words(v_words, vals_words)
         dq_raw = load_rows("dq_raw", dquery, "warm_out")
         g_raw = load_rows("g_raw", gout, "warm_sum")
         load_scales(v_scales, vals_scales)
 
         def interleave(grouped, raw):
-            nc.scalar.copy(out=grouped.rearrange("p (q j) -> p q j", j=PACK), in_=raw[:].rearrange("p j q -> p q j"))
+            nc.scalar.copy(out=grouped.rearrange("p (q t) -> p q t", t=PACK), in_=raw[:].rearrange("p t q -> p q t"))
 
-        def quantize(name, grouped, width):
-            codes = tile(name + "_codes", [P, width], U32)
-            scales = tile(name + "_scales", [P, width], U8)
+        def quantize(name, grouped, operands):
+            codes = tile(name + "_codes", [operands * ROWS], U32)
+            scales = tile(name + "_scales", [operands * ROWS], U8)
             nc.vector.quantize_mx(out=codes[:].bitcast(FP8X4), scales=scales[:], in_=grouped[:])
-            return [(codes[:, c : c + Q], scales[:, c : c + Q]) for c in range(0, width, Q)]
+            return [(codes[:, c : c + ROWS], scales[:, c : c + ROWS]) for c in range(0, operands * ROWS, ROWS)]
 
         def gather(name, pool, dtype):
-            picked = tile(name, [P, SLOTS], dtype)
+            picked = tile(name, [SLOTS], dtype)
             nc.vector.tensor_copy(picked[:], pool[:].indirect(offsets[:]))
             return picked
 
-        def product(name, rows, words, scales):
-            acc = ps.tile([P, SLOTS], F32, name=name)
-            nc.tensor.matmul_mx(out=acc[:], lhsT=rows[0].bitcast(FP8X4), lhsT_scale=rows[1], rhs=words[:].bitcast(FP4X4), rhs_scale=scales[:], start=True, stop=True)
-            return acc
+        def product(acc, rows_mx, words, scales):
+            codes, row_scales = rows_mx
+            nc.tensor.matmul_mx(out=acc, lhsT=codes.bitcast(FP8X4), lhsT_scale=row_scales, rhs=words.bitcast(FP4X4), rhs_scale=scales, start=True, stop=True)
 
-        def col(name):
-            return tile(name, [P, 1], F32)
-
-        def paged(ap):
-            return ap.rearrange("p (g j) -> p g j", j=PAGE)
-
-        def spread(ap):
-            return ap.unsqueeze(2).to_broadcast([P, ap.shape[1], PAGE])
-
-        q_bf = tile("q_bf", [P, Q * PACK], BF16)
-        dg_bf = tile("dg_bf", [P, 2 * Q * PACK], BF16)
+        q_bf = tile("q_bf", [ROWS * PACK], BF16)
+        dg_bf = tile("dg_bf", [2 * ROWS * PACK], BF16)
         interleave(q_bf[:], q_raw)
-        pen_sb = tile("pen_sb", [P, 1], F32, "q_raw")
-        nc.sync.dma_start(out=pen_sb[:], in_=pen)
-        interleave(dg_bf[:, : Q * PACK], dq_raw)
-        interleave(dg_bf[:, Q * PACK :], g_raw)
+        interleave(dg_bf[:, : ROWS * PACK], dq_raw)
+        interleave(dg_bf[:, ROWS * PACK :], g_raw)
 
         kw = gather("kw", k_words, U16)
         ks = gather("ks", k_scales, U8)
-        base_sb = tile("base_sb", [P, T], F32, "k_scales")
-        nc.sync.dma_start(out=base_sb[:], in_=base)
-        (q_mx,) = quantize("q", q_bf, Q)
-        a = product("a", q_mx, kw, ks)
+        pen_sb = tile("pen_sb", [1], on="k_scales")
+        nc.sync.dma_start(out=pen_sb[:], in_=pen)
+        (q_mx,) = quantize("q", q_bf, 1)
+        a = psum.tile([P, SLOTS], F32, name="a")
+        product(a[:], q_mx, kw[:], ks[:])
+
         vw = gather("vw", v_words, U16)
-        neg_max = tile("neg_max", [P, 1], F32, "warm_in")
+        neg_max = tile("neg_max", [1], on="warm_in")
         nc.vector.tensor_reduce(out=neg_max[:], in_=a[:], axis=AXIS.X, op=ALU.max, negate=True)
-        p = tile("p", [P, SLOTS], F32, "warm_sum")
-        z = col("z")
+        p = tile("p", [SLOTS], on="warm_sum")
+        z = tile("z", [1])
         nc.scalar.activation(out=p[:], in_=a[:], func=ACT.Exp, bias=neg_max[:], scale=1.0, accum_out=z[:])
-        vs = gather("vs", v_scales, U8)
-        dq_mx, g_mx = quantize("dg", dg_bf, 2 * Q)
-        ta = product("ta", dq_mx, kw, ks)
-        c0 = product("c0", g_mx, vw, vs)
 
-        held = tile("held", [P, SLOTS + PAGES + 1], F32, "v_scales")
-        tp = held[:, :SLOTS]
-        p_page = held[:, SLOTS : SLOTS + PAGES]
-        rz = held[:, SLOTS + PAGES :]
+        vs = tile("vs", [SLOTS], U8)
+        for h in HALVES:
+            nc.vector.tensor_copy(vs[:, h], v_scales[:].indirect(offsets[:, h.start // LIST_ROWS : h.stop // LIST_ROWS]))
+        dq_mx, g_mx = quantize("dg", dg_bf, 2)
+        ta = psum.tile([P, SLOTS], F32, name="ta")
+        product(ta[:], dq_mx, kw[:], ks[:])
+        c0 = psum.tile([P, SLOTS], F32, name="c0")
+        for h in HALVES:
+            product(c0[:, h], g_mx, vw[:, h], vs[:, h])
+        base_sb = tile("base_sb", [TOKENS], on="kw")
+        nc.sync.dma_start(out=base_sb[:], in_=base)
+
+        p_fours = tile("p_fours", [PAGES, 4], on="dg_bf")
+        nc.gpsimd.tensor_tensor(p_fours[:], paged(p[:])[:, :, 0:4], paged(p[:])[:, :, 4:8], ALU.add)
+        p_twos = tile("p_twos", [PAGES, 2])
+        nc.gpsimd.tensor_tensor(p_twos[:], p_fours[:, :, 0:2], p_fours[:, :, 2:4], ALU.add)
+        p_page = tile("p_page", [PAGES])
+        nc.gpsimd.tensor_tensor(p_page[:], p_twos[:, :, 0], p_twos[:, :, 1], ALU.add)
+
+        after_gathers = tile("after_gathers", [SLOTS + 1], on="v_scales")
+        tp = after_gathers[:, :SLOTS]
+        rz = after_gathers[:, SLOTS:]
         nc.vector.reciprocal(out=rz, in_=z[:])
-        nc.vector.tensor_reduce(out=p_page, in_=paged(p[:]), axis=AXIS.X, op=ALU.add)
-        tz = col("tz")
-        nc.vector.scalar_tensor_tensor(out=tp, in0=ta[:], scalar=1.0, in1=p[:], op0=ALU.mult, op1=ALU.mult, accum_out=tz[:])
 
-        k = col("k")
-        nc.scalar.activation(out=k[:], in_=pen_sb[:], func=ACT.Copy, scale=-2.0)
-        kr = col("kr")
-        nc.scalar.activation(out=kr[:], in_=k[:], func=ACT.Copy, scale=rz)
-        m = col("m")
-        nc.scalar.activation(out=m[:], in_=tz[:], func=ACT.Copy, scale=rz)
-        krp = tile("krp", [P, PAGES], F32)
-        nc.scalar.activation(out=krp[:], in_=p_page, func=ACT.Copy, scale=kr[:])
-        p_sq = tile("p_sq", [P, PAGES], F32)
-        sp2 = col("sp2")
-        nc.scalar.activation(out=p_sq[:], in_=p_page, func=ACT.Square, accum_out=sp2[:])
+        def dot(name, products, psum_side, sbuf_side):
+            total = tile(name, [1])
+            nc.vector.scalar_tensor_tensor(out=products, in0=psum_side[:], scalar=1.0, in1=sbuf_side, op0=ALU.mult, op1=ALU.mult, accum_out=total[:])
+            return total
 
-        pc = tile("pc", [P, SLOTS], F32)
-        c_sum = col("c_sum")
-        nc.vector.scalar_tensor_tensor(out=pc[:], in0=c0[:], scalar=1.0, in1=p[:], op0=ALU.mult, op1=ALU.mult, accum_out=c_sum[:])
-        tp_page = tile("tp_page", [P, PAGES], F32)
-        nc.vector.tensor_reduce(out=tp_page[:], in_=paged(tp), axis=AXIS.X, op=ALU.add)
+        tz = dot("tz", tp, ta, p[:])
 
-        a_sum = col("a_sum")
-        nc.scalar.activation(out=a_sum[:], in_=sp2[:], func=ACT.Identity, scale=kr[:], bias=c_sum[:])
-        a0 = col("a0")
-        nc.scalar.activation(out=a0[:], in_=a_sum[:], func=ACT.Copy, scale=rz)
+        nc.scalar.activation(out=factors[:, 0:1], in_=pen_sb[:], func=ACT.Copy, scale=-4.0)
+        nc.scalar.activation(out=factors[:, 1:2], in_=pen_sb[:], func=ACT.Copy, scale=-2.0)
+        over_z = scaled("over_z", 1 + len(constants), factors[:, 1:], rz)
+        k_rz, two_rz, gain_rz, rz_share = (over_z[:, c : c + 1] for c in range(4))
+        means = scaled("means", 2, over_z[:, 4:6], tz[:])
+        m = means[:, 0:1]
+        neg_m_share = means[:, 1:2]
+        k_s = scaled("k_s", PAGES, p_page[:], k_rz)
+        s_squares = tile("s_squares", [PAGES])
+        s2 = tile("s2", [1])
+        nc.scalar.activation(out=s_squares[:], in_=p_page[:], func=ACT.Square, scale=rz, accum_out=s2[:])
+        k_s2 = scaled("k_s2", 2, factors[:, 0:2], s2[:])
 
-        x1 = tile("x1", [P, SLOTS], F32)
-        nc.vector.scalar_tensor_tensor(out=paged(x1[:]), in0=paged(c0[:]), scalar=a0[:], in1=spread(krp[:]), op0=ALU.subtract, op1=ALU.add)
-        neg_g = tile("neg_g", [P, PAGES], F32)
-        nc.vector.scalar_tensor_tensor(out=neg_g[:], in0=p_page, scalar=m[:], in1=tp_page[:], op0=ALU.mult, op1=ALU.subtract)
-        y = tile("y", [P, SLOTS], F32)
-        e_sum = col("e_sum")
-        nc.vector.scalar_tensor_tensor(out=y[:], in0=ta[:], scalar=m[:], in1=pc[:], op0=ALU.subtract, op1=ALU.mult, accum_out=e_sum[:])
-        gp = tile("gp", [P, PAGES], F32)
-        q2 = col("q2")
-        nc.vector.scalar_tensor_tensor(out=gp[:], in0=neg_g[:], scalar=-2.0, in1=krp[:], op0=ALU.mult, op1=ALU.mult, accum_out=q2[:])
-        x2 = tile("x2", [P, SLOTS], F32)
-        halves = [slice(0, SLOTS // 2), slice(SLOTS // 2, SLOTS)]
-        for h in halves:
-            nc.vector.scalar_tensor_tensor(out=x2[:, h], in0=ta[:, h], scalar=m[:], in1=x1[:, h], op0=ALU.subtract, op1=ALU.mult)
+        p_c0 = tile("p_c0", [SLOTS])
+        tp_c0 = tile("tp_c0", [SLOTS])
+        p_c0_sum = dot("p_c0_sum", p_c0[:], c0, p[:])
+        tp_fours = tile("tp_fours", [PAGES, 4])
+        nc.gpsimd.tensor_tensor(tp_fours[:], paged(tp)[:, :, 0:4], paged(tp)[:, :, 4:8], ALU.add)
+        a0 = affine("a0", p_c0_sum[:], rz, k_s2[:, 1:2])
+        a1 = affine("a1", p_c0_sum[:], rz, k_s2[:, 0:1])
+        tp_c0_sum = dot("tp_c0_sum", tp_c0[:], c0, tp)
+        tp_page = tile("tp_page", [PAGES])
+        nc.vector.tensor_reduce(out=tp_page[:], in_=tp_fours[:], axis=AXIS.X, op=ALU.add)
 
-        neg_krg = tile("neg_krg", [P, PAGES], F32)
-        nc.scalar.activation(out=neg_krg[:], in_=neg_g[:], func=ACT.Copy, scale=kr[:])
-        b_sum = col("b_sum")
-        nc.scalar.activation(out=b_sum[:], in_=q2[:], func=ACT.Identity, scale=1.0, bias=e_sum[:])
-        b0 = col("b0")
-        nc.scalar.activation(out=b0[:], in_=b_sum[:], func=ACT.Copy, scale=rz)
-        gain = col("gain")
-        nc.scalar.activation(out=gain[:], in_=rz, func=ACT.Copy, scale=GAIN)
-        w = tile("w", [P, SLOTS], F32)
-        nc.scalar.activation(out=w[:], in_=p[:], func=ACT.Copy, scale=gain[:])
+        x1 = tile("x1", [SLOTS])
+        for h in HALVES:
+            nc.vector.scalar_tensor_tensor(out=paged(x1[:, h]), in0=paged(c0[:, h]), scalar=a0[:], in1=per_slot(k_s, h), op0=ALU.subtract, op1=ALU.add)
 
-        x3 = tile("x3", [P, SLOTS], F32)
-        for h in halves:
-            nc.vector.scalar_tensor_tensor(out=paged(x3[:, h]), in0=paged(x2[:, h]), scalar=b0[:], in1=spread(neg_krg[:, h.start // PAGE : h.stop // PAGE]), op0=ALU.subtract, op1=ALU.subtract)
-        nc.vector.tensor_tensor(window[:].indirect(offsets[:]), x3[:], w[:], ALU.mult)
+        m_p_page = scaled("m_p_page", PAGES, p_page[:], m)
+        neg_m_a1_share = scaled("neg_m_a1_share", 1, a1[:], neg_m_share)
+        b0_share = affine("b0_share", tp_c0_sum[:], rz_share, neg_m_a1_share[:])
+        neg_ts_z = tile("neg_ts_z", [PAGES])
+        nc.gpsimd.tensor_tensor(neg_ts_z[:], m_p_page[:], tp_page[:], ALU.subtract)
+        k_s_tp = tile("k_s_tp", [PAGES])
+        nc.gpsimd.tensor_tensor(k_s_tp[:], tp_page[:], k_s[:], ALU.mult)
 
-        edges = [0, 256, 768, 1280, 1792, 2048]
-        for c in range(5):
-            cols = slice(edges[c], edges[c + 1])
-            nc.vector.tensor_tensor(result[:, cols], window[:, cols], base_sb[:, cols], ALU.add)
-            nc.sync.dma_start(out=out[:, cols], in_=result[:, cols])
+        x2 = tile("x2", [SLOTS])
+        for h in HALVES:
+            nc.vector.scalar_tensor_tensor(out=x2[:, h], in0=ta[:, h], scalar=m, in1=x1[:, h], op0=ALU.subtract, op1=ALU.mult)
+
+        neg_k_ts = scaled("neg_k_ts", PAGES, neg_ts_z[:], k_rz)
+        b0_terms = tile("b0_terms", [PAGES])
+        b0 = tile("b0", [1])
+        nc.scalar.activation(out=b0_terms[:], in_=k_s_tp[:], func=ACT.Identity, scale=two_rz, bias=b0_share[:], accum_out=b0[:])
+        gain_w = scaled("gain_w", SLOTS, p[:], gain_rz, on="p_c0_sum")
+
+        x3 = tile("x3", [SLOTS])
+        for h in HALVES:
+            nc.vector.scalar_tensor_tensor(out=paged(x3[:, h]), in0=paged(x2[:, h]), scalar=b0[:], in1=per_slot(neg_k_ts, h), op0=ALU.subtract, op1=ALU.subtract)
+
+        nc.vector.tensor_tensor(window[:].indirect(offsets[:]), x3[:], gain_w[:], ALU.mult)
+        for first, last in zip(STORE_EDGES, STORE_EDGES[1:]):
+            nc.vector.tensor_tensor(result[:, first:last], window[:, first:last], base_sb[:, first:last], ALU.add)
+            nc.sync.dma_start(out=out[:, first:last], in_=result[:, first:last])

from contextlib import ExitStack

import concourse.mybir as mybir

F32 = mybir.dt.float32
BF16 = mybir.dt.bfloat16
I32 = mybir.dt.int32
U32 = mybir.dt.uint32
U16 = mybir.dt.uint16
U8 = mybir.dt.uint8
FP8X4 = mybir.dt.float8_e4m3fn_x4
FP4X4 = mybir.dt.float4_e2m1fn_x4
ALU = mybir.AluOpType
ACT = mybir.ActivationFunctionType
AXIS = mybir.AxisListType

P = 128
PACK = 4
QUADRANT = 32
SCALE_ROWS = 16
LIST_ROWS = 16
FEATURES = 512
TOKENS = 2048
SLOTS = 512
ROWS = 128
PAGES = 64
PAGE = SLOTS // PAGES
GAIN = 512.0
HALVES = (slice(0, SLOTS // 2), slice(SLOTS // 2, SLOTS))
STORE_EDGES = (0, 256, 768, 1280, 1792, 2048)
FIRST_CLEAR = 256

FLOPS = 3 * 2 * FEATURES * ROWS * SLOTS


def tile_attend_hvcrowding_s_kernel(tc, query, keys_words, keys_scales, pen, gout, vals_words, vals_scales, dquery, base, offs, out):
    nc = tc.nc
    with ExitStack() as ctx:
        sbuf = ctx.enter_context(tc.tile_pool(name="sbuf", bufs=1))
        psum = ctx.enter_context(tc.psum_pool(name="psum", bufs=1))

        def tile(name, width, dtype=F32, on=None):
            return sbuf.tile([P] + width, dtype, name=name, tag=on or name, align_bytes=64)

        def paged(ap):
            return ap.rearrange("p (g j) -> p g j", j=PAGE)

        def per_slot(page_values, half):
            pages = page_values[:, half.start // PAGE : half.stop // PAGE]
            return pages.unsqueeze(2).to_broadcast([P, PAGES // 2, PAGE])

        def scaled(name, width, src, scale, on=None):
            dst = tile(name, [width], on=on)
            nc.scalar.activation(out=dst[:], in_=src, func=ACT.Copy, scale=scale)
            return dst

        def affine(name, src, scale, bias):
            dst = tile(name, [1])
            nc.scalar.activation(out=dst[:], in_=src, func=ACT.Identity, scale=scale, bias=bias)
            return dst

        offsets = tile("offsets", [SLOTS // LIST_ROWS], U16)
        k_words = tile("k_words", [TOKENS], U16)
        k_scales = tile("k_scales", [TOKENS], U8)
        v_scales = tile("v_scales", [TOKENS], U8)
        window = tile("window", [TOKENS])
        result = tile("result", [TOKENS])

        nc.vector.memset(k_scales[:].bitcast(I32), 0)
        constants = [2.0, GAIN, 1.0 / PAGES, 1.0, -1.0 / PAGES]
        seed = tile("seed", [len(constants)])
        for c, value in enumerate(constants):
            nc.vector.memset(seed[:, c : c + 1], value)
        factors = tile("factors", [2 + len(constants)])
        nc.vector.tensor_copy(factors[:, 2:], seed[:])
        nc.vector.memset(window[:, :FIRST_CLEAR], 0.0)
        nc.vector.memset(window[:, FIRST_CLEAR:], 0.0)
        nc.vector.memset(v_scales[:].bitcast(I32), 0)

        warm_in = tile("warm_in", [1])
        warm_out = tile("warm_out", [1])
        warm_sum = tile("warm_sum", [1])
        nc.gpsimd.memset(warm_in[:], 0.0)
        nc.scalar.activation(out=warm_out[:], in_=warm_in[:], func=ACT.Exp, accum_out=warm_sum[:])

        def load_words(dst, src):
            nc.sync.dma_start(out=dst[:].bitcast(I32), in_=src[0].bitcast(I32))

        def load_scales(dst, src):
            for r in range(PACK):
                nc.sync.dma_start(out=dst[r:P:QUADRANT, :].bitcast(I32), in_=src[0, r:SCALE_ROWS:PACK, :].bitcast(I32))

        def load_rows(name, src, on):
            raw = tile(name, [PACK, ROWS], on=on)
            nc.sync.dma_start(out=raw[:], in_=src.rearrange("(p t) q -> p t q", t=PACK))
            return raw

        nc.sync.dma_start(offsets[:], offs)
        load_words(k_words, keys_words)
        load_scales(k_scales, keys_scales)
        q_raw = load_rows("q_raw", query, "seed")
        v_words = tile("v_words", [TOKENS], U16, on="warm_in")
        load_words(v_words, vals_words)
        dq_raw = load_rows("dq_raw", dquery, "warm_out")
        g_raw = load_rows("g_raw", gout, "warm_sum")
        load_scales(v_scales, vals_scales)

        def interleave(grouped, raw):
            nc.scalar.copy(out=grouped.rearrange("p (q t) -> p q t", t=PACK), in_=raw[:].rearrange("p t q -> p q t"))

        def quantize(name, grouped, operands):
            codes = tile(name + "_codes", [operands * ROWS], U32)
            scales = tile(name + "_scales", [operands * ROWS], U8)
            nc.vector.quantize_mx(out=codes[:].bitcast(FP8X4), scales=scales[:], in_=grouped[:])
            return [(codes[:, c : c + ROWS], scales[:, c : c + ROWS]) for c in range(0, operands * ROWS, ROWS)]

        def gather(name, pool, dtype):
            picked = tile(name, [SLOTS], dtype)
            nc.vector.tensor_copy(picked[:], pool[:].indirect(offsets[:]))
            return picked

        def product(acc, rows_mx, words, scales):
            codes, row_scales = rows_mx
            nc.tensor.matmul_mx(out=acc, lhsT=codes.bitcast(FP8X4), lhsT_scale=row_scales, rhs=words.bitcast(FP4X4), rhs_scale=scales, start=True, stop=True)

        q_bf = tile("q_bf", [ROWS * PACK], BF16)
        dg_bf = tile("dg_bf", [2 * ROWS * PACK], BF16)
        interleave(q_bf[:], q_raw)
        interleave(dg_bf[:, : ROWS * PACK], dq_raw)
        interleave(dg_bf[:, ROWS * PACK :], g_raw)

        kw = gather("kw", k_words, U16)
        ks = gather("ks", k_scales, U8)
        pen_sb = tile("pen_sb", [1], on="k_scales")
        nc.sync.dma_start(out=pen_sb[:], in_=pen)
        (q_mx,) = quantize("q", q_bf, 1)
        a = psum.tile([P, SLOTS], F32, name="a")
        product(a[:], q_mx, kw[:], ks[:])

        vw = gather("vw", v_words, U16)
        neg_max = tile("neg_max", [1], on="warm_in")
        nc.vector.tensor_reduce(out=neg_max[:], in_=a[:], axis=AXIS.X, op=ALU.max, negate=True)
        p = tile("p", [SLOTS], on="warm_sum")
        z = tile("z", [1])
        nc.scalar.activation(out=p[:], in_=a[:], func=ACT.Exp, bias=neg_max[:], scale=1.0, accum_out=z[:])

        vs = tile("vs", [SLOTS], U8)
        for h in HALVES:
            nc.vector.tensor_copy(vs[:, h], v_scales[:].indirect(offsets[:, h.start // LIST_ROWS : h.stop // LIST_ROWS]))
        dq_mx, g_mx = quantize("dg", dg_bf, 2)
        ta = psum.tile([P, SLOTS], F32, name="ta")
        product(ta[:], dq_mx, kw[:], ks[:])
        c0 = psum.tile([P, SLOTS], F32, name="c0")
        for h in HALVES:
            product(c0[:, h], g_mx, vw[:, h], vs[:, h])
        base_sb = tile("base_sb", [TOKENS], on="kw")
        nc.sync.dma_start(out=base_sb[:], in_=base)

        p_fours = tile("p_fours", [PAGES, 4], on="dg_bf")
        nc.gpsimd.tensor_tensor(p_fours[:], paged(p[:])[:, :, 0:4], paged(p[:])[:, :, 4:8], ALU.add)
        p_twos = tile("p_twos", [PAGES, 2])
        nc.gpsimd.tensor_tensor(p_twos[:], p_fours[:, :, 0:2], p_fours[:, :, 2:4], ALU.add)
        p_page = tile("p_page", [PAGES])
        nc.gpsimd.tensor_tensor(p_page[:], p_twos[:, :, 0], p_twos[:, :, 1], ALU.add)

        after_gathers = tile("after_gathers", [SLOTS + 1], on="v_scales")
        tp = after_gathers[:, :SLOTS]
        rz = after_gathers[:, SLOTS:]
        nc.vector.reciprocal(out=rz, in_=z[:])

        def dot(name, products, psum_side, sbuf_side):
            total = tile(name, [1])
            nc.vector.scalar_tensor_tensor(out=products, in0=psum_side[:], scalar=1.0, in1=sbuf_side, op0=ALU.mult, op1=ALU.mult, accum_out=total[:])
            return total

        tz = dot("tz", tp, ta, p[:])

        nc.scalar.activation(out=factors[:, 0:1], in_=pen_sb[:], func=ACT.Copy, scale=-4.0)
        nc.scalar.activation(out=factors[:, 1:2], in_=pen_sb[:], func=ACT.Copy, scale=-2.0)
        over_z = scaled("over_z", 1 + len(constants), factors[:, 1:], rz)
        k_rz, two_rz, gain_rz, rz_share = (over_z[:, c : c + 1] for c in range(4))
        means = scaled("means", 2, over_z[:, 4:6], tz[:])
        m = means[:, 0:1]
        neg_m_share = means[:, 1:2]
        k_s = scaled("k_s", PAGES, p_page[:], k_rz)
        s_squares = tile("s_squares", [PAGES])
        s2 = tile("s2", [1])
        nc.scalar.activation(out=s_squares[:], in_=p_page[:], func=ACT.Square, scale=rz, accum_out=s2[:])
        k_s2 = scaled("k_s2", 2, factors[:, 0:2], s2[:])

        p_c0 = tile("p_c0", [SLOTS])
        tp_c0 = tile("tp_c0", [SLOTS])
        p_c0_sum = dot("p_c0_sum", p_c0[:], c0, p[:])
        tp_fours = tile("tp_fours", [PAGES, 4])
        nc.gpsimd.tensor_tensor(tp_fours[:], paged(tp)[:, :, 0:4], paged(tp)[:, :, 4:8], ALU.add)
        a0 = affine("a0", p_c0_sum[:], rz, k_s2[:, 1:2])
        a1 = affine("a1", p_c0_sum[:], rz, k_s2[:, 0:1])
        tp_c0_sum = dot("tp_c0_sum", tp_c0[:], c0, tp)
        tp_page = tile("tp_page", [PAGES])
        nc.vector.tensor_reduce(out=tp_page[:], in_=tp_fours[:], axis=AXIS.X, op=ALU.add)

        x1 = tile("x1", [SLOTS])
        for h in HALVES:
            nc.vector.scalar_tensor_tensor(out=paged(x1[:, h]), in0=paged(c0[:, h]), scalar=a0[:], in1=per_slot(k_s, h), op0=ALU.subtract, op1=ALU.add)

        m_p_page = scaled("m_p_page", PAGES, p_page[:], m)
        neg_m_a1_share = scaled("neg_m_a1_share", 1, a1[:], neg_m_share)
        b0_share = affine("b0_share", tp_c0_sum[:], rz_share, neg_m_a1_share[:])
        neg_ts_z = tile("neg_ts_z", [PAGES])
        nc.gpsimd.tensor_tensor(neg_ts_z[:], m_p_page[:], tp_page[:], ALU.subtract)
        k_s_tp = tile("k_s_tp", [PAGES])
        nc.gpsimd.tensor_tensor(k_s_tp[:], tp_page[:], k_s[:], ALU.mult)

        x2 = tile("x2", [SLOTS])
        for h in HALVES:
            nc.vector.scalar_tensor_tensor(out=x2[:, h], in0=ta[:, h], scalar=m, in1=x1[:, h], op0=ALU.subtract, op1=ALU.mult)

        neg_k_ts = scaled("neg_k_ts", PAGES, neg_ts_z[:], k_rz)
        b0_terms = tile("b0_terms", [PAGES])
        b0 = tile("b0", [1])
        nc.scalar.activation(out=b0_terms[:], in_=k_s_tp[:], func=ACT.Identity, scale=two_rz, bias=b0_share[:], accum_out=b0[:])
        gain_w = scaled("gain_w", SLOTS, p[:], gain_rz, on="p_c0_sum")

        x3 = tile("x3", [SLOTS])
        for h in HALVES:
            nc.vector.scalar_tensor_tensor(out=paged(x3[:, h]), in0=paged(x2[:, h]), scalar=b0[:], in1=per_slot(neg_k_ts, h), op0=ALU.subtract, op1=ALU.subtract)

        nc.vector.tensor_tensor(window[:].indirect(offsets[:]), x3[:], gain_w[:], ALU.mult)
        for first, last in zip(STORE_EDGES, STORE_EDGES[1:]):
            nc.vector.tensor_tensor(result[:, first:last], window[:, first:last], base_sb[:, first:last], ALU.add)
            nc.sync.dma_start(out=out[:, first:last], in_=result[:, first:last])
